import numpy as np
import ml_dtypes


def mxq(x, axis, fmt="e4m3"):
    dtype, down = {"e4m3": (ml_dtypes.float8_e4m3fn, 7), "e5m2": (ml_dtypes.float8_e5m2, 14)}[fmt]
    v = np.moveaxis(np.asarray(x, np.float32).astype(ml_dtypes.bfloat16).astype(np.float64), axis, -1)
    blocks = v.reshape(v.shape[:-1] + (-1, 32))
    amax = np.abs(blocks).max(-1, keepdims=True)
    byte = np.maximum(np.where(amax > 0, np.frexp(amax)[1] - 1 + 127, 0) - down, 1)
    scale = np.exp2(byte - 127.0)
    codes = (blocks / scale).astype(np.float32).astype(dtype).astype(np.float64)
    return np.moveaxis((codes * scale).reshape(v.shape), -1, axis)


WIDE = False


def mx_kscale(k):
    if not WIDE:
        return np.ones(k)
    levels = np.array([10, -10, 5, -5, 0])
    if k % 512:
        return np.exp2(np.random.permutation(np.resize(levels, k // 32))).repeat(32)
    a = np.empty((k // 512, 16))
    for p in range(k // 512):
        a[p, :8] = np.random.permutation(np.resize(levels, 8))
        for g in range(8):
            far = levels[np.abs(levels - a[p, g]) >= 10]
            a[p, g + 8] = far[np.random.randint(len(far))]
    return np.exp2(a.ravel()).repeat(32)


def f64(x):
    return np.asarray(x).astype(np.float64)


def striped(idx):
    return np.tile(idx.reshape(-1, 16).T, (8, 1)).astype(np.uint16)


def unstriped(offs):
    return offs[:16].T.reshape(-1).astype(np.int64)


def striped8(idx):
    return np.concatenate([x.reshape(-1, 16).T for x in idx]).astype(np.uint16)


def runs(offs, k):
    lists = np.stack([offs[16 * r : 16 * r + 16].T.reshape(-1) for r in range(8)]).astype(np.int64)
    return lists[np.arange(k) % 512 // 64]


def pack_weight(w):
    k, n = w.shape
    w = f64(np.asarray(w, np.float32).astype(ml_dtypes.bfloat16)).reshape(k // 32, 32, n)
    amax = np.abs(w).max(1)
    byte = np.clip(np.where(amax > 0, np.frexp(amax)[1] - 1 + 127 - 7, 1), 1, 254)
    scaled = (w * np.exp2(127.0 - byte)[:, None, :]).reshape(k, n).astype(np.float32)
    words = np.ascontiguousarray(scaled.reshape(k // 512, 128, 4, n).transpose(0, 1, 3, 2)).astype(ml_dtypes.float8_e4m3fn).view(np.uint8)
    return words, np.ascontiguousarray(byte.astype(np.uint8).reshape(k // 512, 16, n))


def unpack_weight(words, scales):
    g, p, n, _ = words.shape
    vals = np.ascontiguousarray(words).view(ml_dtypes.float8_e4m3fn).astype(np.float64) * np.repeat(np.exp2(scales.astype(np.float64) - 127.0), 8, axis=1)[..., None]
    return vals.transpose(0, 1, 3, 2).reshape(g * 512, n)


E2M1 = np.array([0.0, 0.5, 1.0, 1.5, 2.0, 3.0, 4.0, 6.0, -0.0, -0.5, -1.0, -1.5, -2.0, -3.0, -4.0, -6.0])


def pack_fp4(w):
    k, n = w.shape
    w = f64(np.asarray(w, np.float32).astype(ml_dtypes.bfloat16)).reshape(k // 32, 32, n)
    amax = np.abs(w).max(1)
    mant, ex = np.frexp(amax / 6.0)
    byte = np.clip(np.where(amax > 0, np.where(mant > 0.5, ex, ex - 1) + 127, 1), 1, 254)
    scaled = (w * np.exp2(127.0 - byte)[:, None, :]).reshape(k, n).astype(np.float32)
    c = np.ascontiguousarray(scaled.reshape(k // 512, 128, 4, n).transpose(0, 1, 3, 2)).astype(ml_dtypes.float4_e2m1fn).view(np.uint8) & 0xF
    words = (c[..., 0::2] | (c[..., 1::2] << 4)).reshape(k // 512, 128, 2 * n)
    return np.ascontiguousarray(words), np.ascontiguousarray(byte.astype(np.uint8).reshape(k // 512, 16, n))


def unpack_fp4(words, scales):
    g, _, n = scales.shape
    words = np.ascontiguousarray(words).reshape(g, 128, n, 2)
    nib = np.empty((g, 128, n, 4), np.uint8)
    nib[..., 0::2] = words & 0xF
    nib[..., 1::2] = words >> 4
    vals = E2M1[nib] * np.repeat(np.exp2(scales.astype(np.float64) - 127.0), 8, axis=1)[..., None]
    return vals.transpose(0, 1, 3, 2).reshape(g * 512, n)


def sigmoid(v):
    return 1.0 / (1.0 + np.exp(-np.maximum(v, -700.0)))

def planes(y):
    n, m = y.shape
    v = y.astype(np.float32).astype(ml_dtypes.bfloat16).astype(np.float64).reshape(n // 32, 32, m)
    top = np.abs(v).max(1)
    byte = np.clip(np.where(top > 0, np.frexp(top)[1] - 1 + 127 - 7, 1), 1, 254)
    codes = (v * np.exp2(127.0 - byte)[:, None, :]).reshape(n, m).astype(np.float32).astype(ml_dtypes.float8_e4m3fn).view(np.uint8)
    words = codes.reshape(n // 512, 128, 4, m).transpose(0, 1, 3, 2)
    return np.ascontiguousarray(words), np.ascontiguousarray(byte.astype(np.uint8).reshape(n // 512, 16, m))


K, T, S, N, H, G, W = 512, 2048, 512, 512, 512, 2048, 1024


def setup_inputs():
    n = np.random.standard_normal
    s = mx_kscale(K)[:, None]
    u = mx_kscale(S)
    packed_xT = pack_weight(n((K, T)) * s)
    packed_w1 = pack_fp4(n((K, H)) / np.sqrt(K) / s)
    packed_dT = pack_weight(n((K, G)) / s)
    packed_w2 = pack_fp4(n((H, N)) / np.sqrt(H) / u[:, None])
    return {
        "x_words": packed_xT[0],
        "x_scales": packed_xT[1],
        "w1_words": packed_w1[0],
        "w1_scales": packed_w1[1],
        "d_words": packed_dT[0],
        "d_scales": packed_dT[1],
        "gn": (np.random.uniform(0.5, 1.5, (H, 1)) * u[:, None]).astype(np.float32),
        "w2_words": packed_w2[0],
        "w2_scales": packed_w2[1],
        "offs": striped(np.random.permutation(T)[:S]),
        "k1": striped8(np.random.randint(0, G, (8, H))),
        "two": striped(np.random.permutation(T)[:S]),
        "n1": striped8(np.stack([np.random.permutation(S) for _ in range(8)])),
        "n2": striped8(np.stack([np.random.permutation(S) for _ in range(8)])),
        "n3": striped8(np.stack([np.random.permutation(S) for _ in range(8)])),
        "n4": striped8(np.stack([np.random.permutation(S) for _ in range(8)])),
        "n5": striped(np.random.randint(0, S, W)),
    }


def reference(x_words, x_scales, w1_words, w1_scales, d_words, d_scales, gn, w2_words, w2_scales, offs, k1, two, n1, n2, n3, n4, n5):
    xq = unpack_weight(x_words, x_scales)[:, unstriped(offs)]
    y = unpack_fp4(w1_words, w1_scales).T @ xq
    d_k1 = unpack_weight(d_words, d_scales)[np.arange(K)[:, None], runs(k1, K)]
    x_two = unpack_weight(x_words, x_scales)[:, unstriped(two)]
    d = 0.0625 * (d_k1.T @ x_two)
    z = f64(gn) * (np.maximum(y[np.arange(H)[:, None], runs(n1, H)] + d[np.arange(H)[:, None], runs(n3, H)], y[np.arange(H)[:, None], runs(n2, H)] + d[np.arange(H)[:, None], runs(n4, H)]))
    h = unpack_fp4(w2_words, w2_scales).T @ mxq(z, 0, "e4m3")
    mb = h[:, unstriped(n5)]
    mn = mb.reshape(N, S, 2).min(axis=2)
    mx = mb.reshape(N, S, 2).max(axis=2)
    out_0 = (h - mn) * sigmoid(mx)
    return (out_0,) + planes(out_0)

@@ -1,0 +1,259 @@
+from contextlib import ExitStack
+
+import concourse.mybir as mybir
+
+F32 = mybir.dt.float32
+BF16 = mybir.dt.bfloat16
+I32 = mybir.dt.int32
+U32 = mybir.dt.uint32
+U16 = mybir.dt.uint16
+U8 = mybir.dt.uint8
+FP8X4 = mybir.dt.float8_e4m3fn_x4
+FP4X4 = mybir.dt.float4_e2m1fn_x4
+ALU = mybir.AluOpType
+ACT = mybir.ActivationFunctionType
+
+P = 128
+PACK = 4
+TABLE = 2048
+S = 512
+FUSED_UNITS = 5
+XS_SPLIT = 320
+VECTOR_PICKS = 2
+Z_CHUNKS = ((0, 256), (256, 256))
+OUT_CHUNKS = ((0, 128), (128, 128), (256, 128), (384, 128))
+
+FLOPS = 3 * 2 * 512 * 512 * 512
+
+
+def tile_picked_twkeypathbghard_none_po_kernel(
+    tc, x_words, x_scales, w1_words, w1_scales, d_words, d_scales, gn, w2_words, w2_scales,
+    offs, k1, two, n1, n2, n3, n4, n5, out_0, out_1, out_2,
+):
+    nc = tc.nc
+    with ExitStack() as ctx:
+        held = ctx.enter_context(tc.tile_pool(name="held", bufs=1))
+        ring = ctx.enter_context(tc.tile_pool(name="ring", bufs=3))
+        psum = ctx.enter_context(tc.psum_pool(name="psum", bufs=1))
+
+        def tile(shape, dtype, name, tag=None):
+            return held.tile(shape, dtype, name=name, tag=tag or name, align_bytes=64)
+
+        def load_list(src, name):
+            t = tile([P, src.shape[1]], U16, name)
+            nc.sync.dma_start(t[:], src)
+            return t
+
+        def zeroed_bytes(engine, width, name):
+            t = tile([P, width], U8, name)
+            engine.memset(t[:].bitcast(I32), 0)
+            return t
+
+        def load_scale_rows(queue, dst, src, rows):
+            for a in range(PACK):
+                queue.dma_start(dst[:].bitcast(I32)[rows[a] : P : 32, :], src[0].bitcast(I32)[a : 16 : PACK, :])
+
+        def load_words(src, name):
+            t = tile([P, TABLE], U32, name)
+            nc.sync.dma_start(t[:].bitcast(I32), src[0].rearrange("p c r -> p (c r)").bitcast(I32))
+            return t
+
+        def load_fp4(src, name):
+            t = tile([P, 2 * S], U8, name)
+            nc.sync.dma_start(t[:].bitcast(I32), src[0].bitcast(I32))
+            return t
+
+        def gather(table, offsets, dtype, name, tag=None):
+            t = tile([P, S], dtype, name, tag)
+            nc.vector.tensor_copy(t[:], table[:].indirect(offsets[:]))
+            return t
+
+        def deal(src, dtype, size, name, tag=None):
+            t = tile([P, S * size], dtype, name, tag)
+            nc.vector.tensor_copy(
+                t[:].rearrange("p (t m b) -> p t m b", t=PACK, b=size),
+                src[:].rearrange("p (m t b) -> p t m b", t=PACK, b=size),
+            )
+            return t
+
+        xs = tile([P, TABLE], U8, "xs")
+        nc.vector.memset(xs[:].bitcast(I32)[:, :XS_SPLIT], 0)
+        nc.gpsimd.memset(xs[:].bitcast(I32)[:, XS_SPLIT:], 0)
+        w1s = zeroed_bytes(nc.vector, S, "w1s")
+        ds = zeroed_bytes(nc.vector, TABLE, "ds")
+        w2s = zeroed_bytes(nc.vector, S, "w2s")
+        offs_t = load_list(offs, "offs_t")
+        two_t = load_list(two, "two_t")
+        w1w = load_fp4(w1_words, "w1w")
+        load_scale_rows(nc.sync, xs, x_scales, range(PACK))
+        xw = load_words(x_words, "xw")
+        load_scale_rows(nc.sync, w1s, w1_scales, range(PACK))
+        k1_t = load_list(k1, "k1_t")
+        nc.sync.dma_start(ds[:].bitcast(I32)[0:P:8, :], d_scales[0].bitcast(I32))
+        n1_t = load_list(n1, "n1_t")
+        dw = load_words(d_words, "dw")
+        n2_t = load_list(n2, "n2_t")
+        n3_t = load_list(n3, "n3_t")
+        n4_t = load_list(n4, "n4_t")
+        gain = tile([P, PACK], F32, "gain")
+        nc.sync.dma_start(gain[:], gn.rearrange("(p t) o -> p (t o)", t=PACK))
+        w2w = load_fp4(w2_words, "w2w")
+        n5_t = load_list(n5, "n5_t")
+        load_scale_rows(nc.sync, w2s, w2_scales, range(PACK))
+
+        h = [tile([P, S], F32, "h%d" % t) for t in range(PACK)]
+
+        w1w_d = deal(w1w, U8, 2, "w1w_d")
+        x1s = gather(xs, offs_t, U8, "x1s")
+        x1w = gather(xw, offs_t, U32, "x1w")
+        w1s_d = deal(w1s, U8, 1, "w1s_d")
+        y = []
+        for t in range(PACK):
+            bank = psum.tile([P, S], F32, name="bank_a%d" % t)
+            nc.tensor.matmul_mx(
+                out=bank[:], lhsT=w1w_d[:, 2 * P * t : 2 * P * (t + 1)].bitcast(FP4X4), lhsT_scale=w1s_d[:, P * t : P * (t + 1)],
+                rhs=x1w[:].bitcast(FP8X4), rhs_scale=x1s[:], start=True, stop=True,
+            )
+            y_t = tile([P, S], F32, "y%d" % t)
+            nc.scalar.activation(y_t[:], bank[:], ACT.Copy)
+            y.append(y_t)
+
+        dks = gather(ds, k1_t, U8, "dks")
+        dks_d = deal(dks, U8, 1, "dks_d")
+        dks_p = tile([P, S], U8, "dks_p")
+        nc.vector.tensor_copy(dks_p[:].bitcast(I32), dks_d[:].bitcast(I32))
+        for a in range(1, PACK):
+            nc.sync.dma_start(dks_p[:].bitcast(I32)[a:P:32, :], dks_d[:].bitcast(I32)[8 * a : P : 32, :])
+        x2s = gather(xs, two_t, U8, "x2s")
+        x2w = gather(xw, two_t, U32, "x2w")
+        dkw = gather(dw, k1_t, U32, "dkw")
+        dkw_d = deal(dkw, U32, 1, "dkw_d")
+        w2w_d = deal(w2w, U8, 2, "w2w_d", "dkw")
+        w2s_d = deal(w2s, U8, 1, "w2s_d", "dw")
+        d = []
+        for t in range(PACK):
+            bank = psum.tile([P, S], F32, name="bank_b%d" % t)
+            nc.tensor.matmul_mx(
+                out=bank[:], lhsT=dkw_d[:, P * t : P * (t + 1)].bitcast(FP8X4), lhsT_scale=dks_p[:, P * t : P * (t + 1)],
+                rhs=x2w[:].bitcast(FP8X4), rhs_scale=x2s[:], start=True, stop=True,
+            )
+            d_t = tile([P, S], F32, "d%d" % t)
+            nc.vector.tensor_scalar(d_t[:], bank[:], 0.0625, None, ALU.mult)
+            d.append(d_t)
+
+        units = [(c, t) for c in range(len(Z_CHUNKS)) for t in range(PACK)]
+        picked = {}
+        z_rows = [tile([P, PACK, width], BF16, "z_rows%d" % c) for c, (start, width) in enumerate(Z_CHUNKS)]
+
+        def columns(offsets, start, count):
+            return offsets[:, start // 16 : (start + count) // 16]
+
+        def pick_y(c, t):
+            start, width = Z_CHUNKS[c]
+            g = tile([P, 2, width], F32, "ypick%d_%d" % (c, t))
+            for e, offsets in enumerate((n1_t, n2_t)):
+                nc.scalar.activation(g[:, e, :], y[t][:].indirect(columns(offsets, start, width)), ACT.Copy)
+            picked[c, t] = g
+            if PACK * c + t >= FUSED_UNITS:
+                g = tile([P, 2, width], F32, "dpick%d_%d" % (c, t))
+                for e, offsets in enumerate((n3_t, n4_t)):
+                    nc.scalar.activation(g[:, e, :], d[t][:].indirect(columns(offsets, start, width)), ACT.Copy)
+                picked[c, t, "d"] = g
+
+        def make_z(c, t):
+            start, width = Z_CHUNKS[c]
+            sums = tile([P, 2, width], F32, "sums%d_%d" % (c, t))
+            if (c, t, "d") in picked:
+                nc.vector.tensor_tensor(sums[:], picked[c, t, "d"][:], picked[c, t][:], ALU.add)
+            else:
+                for e, offsets in enumerate((n3_t, n4_t)):
+                    nc.vector.tensor_tensor(sums[:, e, :], d[t][:].indirect(columns(offsets, start, width)), picked[c, t][:, e, :], ALU.add)
+            top = tile([P, width], F32, "top%d_%d" % (c, t))
+            nc.vector.tensor_tensor(top[:], sums[:, 0, :], sums[:, 1, :], ALU.max)
+            nc.scalar.activation(z_rows[c][:, t, :], top[:], ACT.Copy, scale=gain[:, t : t + 1])
+
+        def make_h(c):
+            start, width = Z_CHUNKS[c]
+            z_in = tile([P, width, PACK], BF16, "z_in%d" % c)
+            nc.vector.tensor_copy(z_in[:], z_rows[c][:].rearrange("p t j -> p j t"))
+            zw = tile([P, width], U32, "zw%d" % c)
+            zs = tile([P, width], U8, "zs%d" % c)
+            nc.vector.quantize_mx(out=zw[:].bitcast(FP8X4), scales=zs[:], in_=z_in[:].rearrange("p j t -> p (j t)"))
+            for t in range(PACK):
+                bank = psum.tile([P, S], F32, name="bank_%s%d" % ("ab"[c % 2], t))
+                nc.tensor.matmul_mx(
+                    out=bank[:, :width], lhsT=w2w_d[:, 2 * P * t : 2 * P * (t + 1)].bitcast(FP4X4), lhsT_scale=w2s_d[:, P * t : P * (t + 1)],
+                    rhs=zw[:].bitcast(FP8X4), rhs_scale=zs[:], start=True, stop=True,
+                )
+                nc.scalar.activation(h[t][:, start : start + width], bank[:, :width], ACT.Copy, scale=0.5)
+
+        ahead = 2
+        for u in range(ahead):
+            pick_y(*units[u])
+        for u, (c, t) in enumerate(units):
+            if u + ahead < len(units):
+                pick_y(*units[u + ahead])
+            make_z(c, t)
+            if t == 0 and c > 0:
+                make_h(c - 1)
+        make_h(len(Z_CHUNKS) - 1)
+
+        out_rows = out_0.rearrange("(p t) j -> p t j", t=PACK)
+        out_words = out_1[0].rearrange("p c r -> p (c r)").bitcast(I32)
+        ow = tile([P, S], U32, "ow")
+        osc = tile([P, S], U8, "osc")
+        last = len(OUT_CHUNKS) - 1
+        units = [(c, 0, PACK) for c in range(last)] + [(last, 0, 2), (last, 2, 2)]
+        result = [tile([P, PACK, width], F32, "result%d" % c) for c, (start, width) in enumerate(OUT_CHUNKS)]
+        members = {}
+
+        def pick_h(u):
+            c, first, count = units[u]
+            start, width = OUT_CHUNKS[c]
+            mb = ring.tile([P, count, 2 * width], F32, name="mb", align_bytes=64, bufs=2)
+            for i in range(count):
+                window = h[first + i][:].indirect(columns(n5_t, 2 * start, 2 * width))
+                if u == 0 and i < VECTOR_PICKS:
+                    nc.vector.tensor_copy(mb[:, i, :], window)
+                else:
+                    nc.scalar.activation(mb[:, i, :], window, ACT.Copy)
+            members[u] = mb
+
+        def gate(u):
+            c, first, count = units[u]
+            start, width = OUT_CHUNKS[c]
+            pairs = members[u][:].rearrange("p t (j e) -> p e t j", e=2)
+            high = ring.tile([P, count, width], F32, name="high", align_bytes=64)
+            low = ring.tile([P, count, width], F32, name="low", align_bytes=64)
+            nc.vector.tensor_tensor(high[:], pairs[:, 0], pairs[:, 1], ALU.max)
+            nc.vector.tensor_tensor(low[:], pairs[:, 0], pairs[:, 1], ALU.min)
+            sig = ring.tile([P, count, width], F32, name="sig", align_bytes=64)
+            nc.scalar.activation(sig[:], high[:], ACT.Tanh)
+            rest = ring.tile([P, count, width], F32, name="rest", align_bytes=64)
+            for i in range(count):
+                nc.vector.tensor_tensor(rest[:, i, :], h[first + i][:, start : start + width], low[:, i, :], ALU.subtract)
+            return rest, sig
+
+        def finish(u, rest, sig):
+            c, first, count = units[u]
+            nc.vector.scalar_tensor_tensor(result[c][:, first : first + count, :], sig[:], 1.0, rest[:], ALU.add, ALU.mult)
+
+        def hand_out(c):
+            start, width = OUT_CHUNKS[c]
+            cols = slice(start, start + width)
+            nc.sync.dma_start(out_rows[:, :, cols], result[c][:])
+            o_in = tile([P, width, PACK], BF16, "o_in%d" % c)
+            nc.vector.tensor_copy(o_in[:], result[c][:].rearrange("p t j -> p j t"))
+            nc.vector.quantize_mx(out=ow[:, cols].bitcast(FP8X4), scales=osc[:, cols], in_=o_in[:].rearrange("p j t -> p (j t)"))
+            nc.sync.dma_start(out_words[:, cols], ow[:, cols].bitcast(I32))
+
+        pick_h(0)
+        for u, (c, first, count) in enumerate(units):
+            if u + 1 < len(units):
+                pick_h(u + 1)
+            finish(u, *gate(u))
+            if first + count == PACK:
+                hand_out(c)
+        for q in range(PACK):
+            queue = nc.sync if q % 2 else nc.scalar
+            queue.dma_start(out_2[0].bitcast(I32)[PACK * q : PACK * (q + 1), :], osc[:].bitcast(I32)[32 * q : 32 * q + PACK, :])

@@ -20,6 +20,7 @@ S = 512
 FUSED_UNITS = 5
 XS_SPLIT = 320
 VECTOR_PICKS = 2
+VECTOR_BANKS = 2
 Z_CHUNKS = ((0, 256), (256, 256))
 OUT_CHUNKS = ((0, 128), (128, 128), (256, 128), (384, 128))
 
@@ -76,6 +77,11 @@ def tile_picked_twkeypathbghard_none_po_kernel(
             )
             return t
 
+        def interleave(dst, src):
+            nc.vector.tensor_copy(
+                dst[:].rearrange("p (c i) t -> p c t i", i=PACK), src[:].rearrange("p t (c i) -> p c t i", i=PACK)
+            )
+
         xs = tile([P, TABLE], U8, "xs")
         nc.vector.memset(xs[:].bitcast(I32)[:, :XS_SPLIT], 0)
         nc.gpsimd.memset(xs[:].bitcast(I32)[:, XS_SPLIT:], 0)
@@ -83,13 +89,13 @@ def tile_picked_twkeypathbghard_none_po_kernel(
         ds = zeroed_bytes(nc.vector, TABLE, "ds")
         w2s = zeroed_bytes(nc.vector, S, "w2s")
         offs_t = load_list(offs, "offs_t")
-        two_t = load_list(two, "two_t")
+        k1_t = load_list(k1, "k1_t")
         w1w = load_fp4(w1_words, "w1w")
         load_scale_rows(nc.sync, xs, x_scales, range(PACK))
         xw = load_words(x_words, "xw")
         load_scale_rows(nc.sync, w1s, w1_scales, range(PACK))
-        k1_t = load_list(k1, "k1_t")
         nc.sync.dma_start(ds[:].bitcast(I32)[0:P:8, :], d_scales[0].bitcast(I32))
+        two_t = load_list(two, "two_t")
         n1_t = load_list(n1, "n1_t")
         dw = load_words(d_words, "dw")
         n2_t = load_list(n2, "n2_t")
@@ -175,7 +181,7 @@ def tile_picked_twkeypathbghard_none_po_kernel(
         def make_h(c):
             start, width = Z_CHUNKS[c]
             z_in = tile([P, width, PACK], BF16, "z_in%d" % c)
-            nc.vector.tensor_copy(z_in[:], z_rows[c][:].rearrange("p t j -> p j t"))
+            interleave(z_in, z_rows[c])
             zw = tile([P, width], U32, "zw%d" % c)
             zs = tile([P, width], U8, "zs%d" % c)
             nc.vector.quantize_mx(out=zw[:].bitcast(FP8X4), scales=zs[:], in_=z_in[:].rearrange("p j t -> p (j t)"))
@@ -185,7 +191,10 @@ def tile_picked_twkeypathbghard_none_po_kernel(
                     out=bank[:, :width], lhsT=w2w_d[:, 2 * P * t : 2 * P * (t + 1)].bitcast(FP4X4), lhsT_scale=w2s_d[:, P * t : P * (t + 1)],
                     rhs=zw[:].bitcast(FP8X4), rhs_scale=zs[:], start=True, stop=True,
                 )
-                nc.scalar.activation(h[t][:, start : start + width], bank[:, :width], ACT.Copy, scale=0.5)
+                if c == len(Z_CHUNKS) - 1 and t < VECTOR_BANKS:
+                    nc.vector.tensor_scalar(h[t][:, start : start + width], bank[:, :width], 0.5, None, ALU.mult)
+                else:
+                    nc.scalar.activation(h[t][:, start : start + width], bank[:, :width], ACT.Copy, scale=0.5)
 
         ahead = 2
         for u in range(ahead):
@@ -194,9 +203,8 @@ def tile_picked_twkeypathbghard_none_po_kernel(
             if u + ahead < len(units):
                 pick_y(*units[u + ahead])
             make_z(c, t)
-            if t == 0 and c > 0:
-                make_h(c - 1)
-        make_h(len(Z_CHUNKS) - 1)
+        for c in range(len(Z_CHUNKS)):
+            make_h(c)
 
         out_rows = out_0.rearrange("(p t) j -> p t j", t=PACK)
         out_words = out_1[0].rearrange("p c r -> p (c r)").bitcast(I32)
@@ -225,8 +233,8 @@ def tile_picked_twkeypathbghard_none_po_kernel(
             pairs = members[u][:].rearrange("p t (j e) -> p e t j", e=2)
             high = ring.tile([P, count, width], F32, name="high", align_bytes=64)
             low = ring.tile([P, count, width], F32, name="low", align_bytes=64)
-            nc.vector.tensor_tensor(high[:], pairs[:, 0], pairs[:, 1], ALU.max)
             nc.vector.tensor_tensor(low[:], pairs[:, 0], pairs[:, 1], ALU.min)
+            nc.vector.tensor_tensor(high[:], pairs[:, 0], pairs[:, 1], ALU.max)
             sig = ring.tile([P, count, width], F32, name="sig", align_bytes=64)
             nc.scalar.activation(sig[:], high[:], ACT.Tanh)
             rest = ring.tile([P, count, width], F32, name="rest", align_bytes=64)
@@ -243,7 +251,7 @@ def tile_picked_twkeypathbghard_none_po_kernel(
             cols = slice(start, start + width)
             nc.sync.dma_start(out_rows[:, :, cols], result[c][:])
             o_in = tile([P, width, PACK], BF16, "o_in%d" % c)
-            nc.vector.tensor_copy(o_in[:], result[c][:].rearrange("p t j -> p j t"))
+            interleave(o_in, result[c])
             nc.vector.quantize_mx(out=ow[:, cols].bitcast(FP8X4), scales=osc[:, cols], in_=o_in[:].rearrange("p j t -> p (j t)"))
             nc.sync.dma_start(out_words[:, cols], ow[:, cols].bitcast(I32))
 
@@ -251,9 +259,11 @@ def tile_picked_twkeypathbghard_none_po_kernel(
         for u, (c, first, count) in enumerate(units):
             if u + 1 < len(units):
                 pick_h(u + 1)
-            finish(u, *gate(u))
-            if first + count == PACK:
-                hand_out(c)
+            made = gate(u)
+            if first == 0 and c > 0:
+                hand_out(c - 1)
+            finish(u, *made)
+        hand_out(last)
         for q in range(PACK):
             queue = nc.sync if q % 2 else nc.scalar
             queue.dma_start(out_2[0].bitcast(I32)[PACK * q : PACK * (q + 1), :], osc[:].bitcast(I32)[32 * q : 32 * q + PACK, :])

@@ -17,12 +17,12 @@ P = 128
 PACK = 4
 TABLE = 2048
 S = 512
-FUSED_UNITS = 5
+FUSED_UNITS = 6
 XS_SPLIT = 320
 VECTOR_PICKS = 2
 VECTOR_BANKS = 2
 Z_CHUNKS = ((0, 256), (256, 256))
-OUT_CHUNKS = ((0, 128), (128, 128), (256, 128), (384, 128))
+OUT_CHUNKS = ((0, 128), (128, 128), (256, 128), (384, 64), (448, 64))
 
 FLOPS = 3 * 2 * 512 * 512 * 512
 
@@ -50,9 +50,9 @@ def tile_picked_twkeypathbghard_none_po_kernel(
             engine.memset(t[:].bitcast(I32), 0)
             return t
 
-        def load_scale_rows(queue, dst, src, rows):
+        def load_scale_rows(queues, dst, src):
             for a in range(PACK):
-                queue.dma_start(dst[:].bitcast(I32)[rows[a] : P : 32, :], src[0].bitcast(I32)[a : 16 : PACK, :])
+                queues[a % len(queues)].dma_start(dst[:].bitcast(I32)[a:P:32, :], src[0].bitcast(I32)[a : 16 : PACK, :])
 
         def load_words(src, name):
             t = tile([P, TABLE], U32, name)
@@ -60,7 +60,7 @@ def tile_picked_twkeypathbghard_none_po_kernel(
             return t
 
         def load_fp4(src, name):
-            t = tile([P, 2 * S], U8, name)
+            t = tile([P, S], U16, name)
             nc.sync.dma_start(t[:].bitcast(I32), src[0].bitcast(I32))
             return t
 
@@ -69,11 +69,11 @@ def tile_picked_twkeypathbghard_none_po_kernel(
             nc.vector.tensor_copy(t[:], table[:].indirect(offsets[:]))
             return t
 
-        def deal(src, dtype, size, name, tag=None):
-            t = tile([P, S * size], dtype, name, tag)
+        def deal(src, dtype, name, tag=None):
+            t = tile([P, S], dtype, name, tag)
             nc.vector.tensor_copy(
-                t[:].rearrange("p (t m b) -> p t m b", t=PACK, b=size),
-                src[:].rearrange("p (m t b) -> p t m b", t=PACK, b=size),
+                t[:].rearrange("p (t m) -> p t m", t=PACK),
+                src[:].rearrange("p (m t) -> p t m", t=PACK),
             )
             return t
 
@@ -88,12 +88,13 @@ def tile_picked_twkeypathbghard_none_po_kernel(
         w1s = zeroed_bytes(nc.vector, S, "w1s")
         ds = zeroed_bytes(nc.vector, TABLE, "ds")
         w2s = zeroed_bytes(nc.vector, S, "w2s")
+        dks_p = zeroed_bytes(nc.vector, S, "dks_p")
         offs_t = load_list(offs, "offs_t")
         k1_t = load_list(k1, "k1_t")
         w1w = load_fp4(w1_words, "w1w")
-        load_scale_rows(nc.sync, xs, x_scales, range(PACK))
+        load_scale_rows((nc.sync, nc.scalar), xs, x_scales)
         xw = load_words(x_words, "xw")
-        load_scale_rows(nc.sync, w1s, w1_scales, range(PACK))
+        load_scale_rows((nc.sync,), w1s, w1_scales)
         nc.sync.dma_start(ds[:].bitcast(I32)[0:P:8, :], d_scales[0].bitcast(I32))
         two_t = load_list(two, "two_t")
         n1_t = load_list(n1, "n1_t")
@@ -105,19 +106,19 @@ def tile_picked_twkeypathbghard_none_po_kernel(
         nc.sync.dma_start(gain[:], gn.rearrange("(p t) o -> p (t o)", t=PACK))
         w2w = load_fp4(w2_words, "w2w")
         n5_t = load_list(n5, "n5_t")
-        load_scale_rows(nc.sync, w2s, w2_scales, range(PACK))
+        load_scale_rows((nc.sync,), w2s, w2_scales)
 
         h = [tile([P, S], F32, "h%d" % t) for t in range(PACK)]
 
-        w1w_d = deal(w1w, U8, 2, "w1w_d")
+        w1w_d = deal(w1w, U16, "w1w_d")
         x1s = gather(xs, offs_t, U8, "x1s")
         x1w = gather(xw, offs_t, U32, "x1w")
-        w1s_d = deal(w1s, U8, 1, "w1s_d")
+        w1s_d = deal(w1s, U8, "w1s_d")
         y = []
         for t in range(PACK):
             bank = psum.tile([P, S], F32, name="bank_a%d" % t)
             nc.tensor.matmul_mx(
-                out=bank[:], lhsT=w1w_d[:, 2 * P * t : 2 * P * (t + 1)].bitcast(FP4X4), lhsT_scale=w1s_d[:, P * t : P * (t + 1)],
+                out=bank[:], lhsT=w1w_d[:, P * t : P * (t + 1)].bitcast(FP4X4), lhsT_scale=w1s_d[:, P * t : P * (t + 1)],
                 rhs=x1w[:].bitcast(FP8X4), rhs_scale=x1s[:], start=True, stop=True,
             )
             y_t = tile([P, S], F32, "y%d" % t)
@@ -125,17 +126,15 @@ def tile_picked_twkeypathbghard_none_po_kernel(
             y.append(y_t)
 
         dks = gather(ds, k1_t, U8, "dks")
-        dks_d = deal(dks, U8, 1, "dks_d")
-        dks_p = tile([P, S], U8, "dks_p")
-        nc.vector.tensor_copy(dks_p[:].bitcast(I32), dks_d[:].bitcast(I32))
-        for a in range(1, PACK):
+        dks_d = deal(dks, U8, "dks_d")
+        for a in range(PACK):
             nc.sync.dma_start(dks_p[:].bitcast(I32)[a:P:32, :], dks_d[:].bitcast(I32)[8 * a : P : 32, :])
         x2s = gather(xs, two_t, U8, "x2s")
         x2w = gather(xw, two_t, U32, "x2w")
         dkw = gather(dw, k1_t, U32, "dkw")
-        dkw_d = deal(dkw, U32, 1, "dkw_d")
-        w2w_d = deal(w2w, U8, 2, "w2w_d", "dkw")
-        w2s_d = deal(w2s, U8, 1, "w2s_d", "dw")
+        dkw_d = deal(dkw, U32, "dkw_d")
+        w2w_d = deal(w2w, U16, "w2w_d", "dkw")
+        w2s_d = deal(w2s, U8, "w2s_d", "dw")
         d = []
         for t in range(PACK):
             bank = psum.tile([P, S], F32, name="bank_b%d" % t)
@@ -188,7 +187,7 @@ def tile_picked_twkeypathbghard_none_po_kernel(
             for t in range(PACK):
                 bank = psum.tile([P, S], F32, name="bank_%s%d" % ("ab"[c % 2], t))
                 nc.tensor.matmul_mx(
-                    out=bank[:, :width], lhsT=w2w_d[:, 2 * P * t : 2 * P * (t + 1)].bitcast(FP4X4), lhsT_scale=w2s_d[:, P * t : P * (t + 1)],
+                    out=bank[:, :width], lhsT=w2w_d[:, P * t : P * (t + 1)].bitcast(FP4X4), lhsT_scale=w2s_d[:, P * t : P * (t + 1)],
                     rhs=zw[:].bitcast(FP8X4), rhs_scale=zs[:], start=True, stop=True,
                 )
                 if c == len(Z_CHUNKS) - 1 and t < VECTOR_BANKS:
@@ -211,7 +210,7 @@ def tile_picked_twkeypathbghard_none_po_kernel(
         ow = tile([P, S], U32, "ow")
         osc = tile([P, S], U8, "osc")
         last = len(OUT_CHUNKS) - 1
-        units = [(c, 0, PACK) for c in range(last)] + [(last, 0, 2), (last, 2, 2)]
+        units = [(c, 0, PACK) for c in range(last + 1)]
         result = [tile([P, PACK, width], F32, "result%d" % c) for c, (start, width) in enumerate(OUT_CHUNKS)]
         members = {}
 

@@ -15,14 +15,19 @@ ACT = mybir.ActivationFunctionType
 
 P = 128
 PACK = 4
+QUADRANT = 32
+LIST_ROWS = 16
 TABLE = 2048
 S = 512
-FUSED_UNITS = 6
-XS_SPLIT = 320
-VECTOR_PICKS = 2
-VECTOR_BANKS = 2
+
 Z_CHUNKS = ((0, 256), (256, 256))
 OUT_CHUNKS = ((0, 128), (128, 128), (256, 128), (384, 64), (448, 64))
+
+XS_SPLIT = 320
+FUSED_STEPS = 5
+VECTOR_BANKS = 2
+VECTOR_PICKS = 2
+PICK_AHEAD = 2
 
 FLOPS = 3 * 2 * 512 * 512 * 512
 
@@ -41,228 +46,232 @@ def tile_picked_twkeypathbghard_none_po_kernel(
             return held.tile(shape, dtype, name=name, tag=tag or name, align_bytes=64)
 
         def load_list(src, name):
-            t = tile([P, src.shape[1]], U16, name)
-            nc.sync.dma_start(t[:], src)
-            return t
+            dst = tile([P, src.shape[1]], U16, name)
+            nc.sync.dma_start(dst[:], src)
+            return dst
 
-        def zeroed_bytes(engine, width, name):
-            t = tile([P, width], U8, name)
-            engine.memset(t[:].bitcast(I32), 0)
-            return t
+        def zeroed_bytes(width, name):
+            dst = tile([P, width], U8, name)
+            nc.vector.memset(dst[:].bitcast(I32), 0)
+            return dst
 
         def load_scale_rows(queues, dst, src):
             for a in range(PACK):
-                queues[a % len(queues)].dma_start(dst[:].bitcast(I32)[a:P:32, :], src[0].bitcast(I32)[a : 16 : PACK, :])
+                queues[a % len(queues)].dma_start(
+                    dst[:].bitcast(I32)[a:P:QUADRANT, :], src[0].bitcast(I32)[a : PACK * PACK : PACK, :]
+                )
 
-        def load_words(src, name):
-            t = tile([P, TABLE], U32, name)
-            nc.sync.dma_start(t[:].bitcast(I32), src[0].rearrange("p c r -> p (c r)").bitcast(I32))
-            return t
+        def load_table_words(src, name):
+            dst = tile([P, TABLE], U32, name)
+            nc.sync.dma_start(dst[:].bitcast(I32), src[0].rearrange("p c r -> p (c r)").bitcast(I32))
+            return dst
 
-        def load_fp4(src, name):
-            t = tile([P, S], U16, name)
-            nc.sync.dma_start(t[:].bitcast(I32), src[0].bitcast(I32))
-            return t
+        def load_weight_words(src, name):
+            dst = tile([P, S], U16, name)
+            nc.sync.dma_start(dst[:].bitcast(I32), src[0].bitcast(I32))
+            return dst
 
-        def gather(table, offsets, dtype, name, tag=None):
-            t = tile([P, S], dtype, name, tag)
-            nc.vector.tensor_copy(t[:], table[:].indirect(offsets[:]))
-            return t
+        def gather_packed(table, offsets, dtype, name):
+            dst = tile([P, S], dtype, name)
+            nc.vector.tensor_copy(dst[:], table[:].indirect(offsets[:]))
+            return dst
 
         def deal(src, dtype, name, tag=None):
-            t = tile([P, S], dtype, name, tag)
+            dst = tile([P, S], dtype, name, tag)
             nc.vector.tensor_copy(
-                t[:].rearrange("p (t m) -> p t m", t=PACK),
+                dst[:].rearrange("p (t m) -> p t m", t=PACK),
                 src[:].rearrange("p (m t) -> p t m", t=PACK),
             )
-            return t
+            return dst
 
         def interleave(dst, src):
             nc.vector.tensor_copy(
                 dst[:].rearrange("p (c i) t -> p c t i", i=PACK), src[:].rearrange("p t (c i) -> p c t i", i=PACK)
             )
 
-        xs = tile([P, TABLE], U8, "xs")
-        nc.vector.memset(xs[:].bitcast(I32)[:, :XS_SPLIT], 0)
-        nc.gpsimd.memset(xs[:].bitcast(I32)[:, XS_SPLIT:], 0)
-        w1s = zeroed_bytes(nc.vector, S, "w1s")
-        ds = zeroed_bytes(nc.vector, TABLE, "ds")
-        w2s = zeroed_bytes(nc.vector, S, "w2s")
-        dks_p = zeroed_bytes(nc.vector, S, "dks_p")
-        offs_t = load_list(offs, "offs_t")
-        k1_t = load_list(k1, "k1_t")
-        w1w = load_fp4(w1_words, "w1w")
-        load_scale_rows((nc.sync, nc.scalar), xs, x_scales)
-        xw = load_words(x_words, "xw")
-        load_scale_rows((nc.sync,), w1s, w1_scales)
-        nc.sync.dma_start(ds[:].bitcast(I32)[0:P:8, :], d_scales[0].bitcast(I32))
-        two_t = load_list(two, "two_t")
-        n1_t = load_list(n1, "n1_t")
-        dw = load_words(d_words, "dw")
-        n2_t = load_list(n2, "n2_t")
-        n3_t = load_list(n3, "n3_t")
-        n4_t = load_list(n4, "n4_t")
+        def product(out, words, dtype, scales, t, rhs_words, rhs_scales):
+            nc.tensor.matmul_mx(
+                out=out, lhsT=words[:, P * t : P * (t + 1)].bitcast(dtype), lhsT_scale=scales[:, P * t : P * (t + 1)],
+                rhs=rhs_words[:].bitcast(FP8X4), rhs_scale=rhs_scales[:], start=True, stop=True,
+            )
+
+        def entries(offsets, start, count):
+            return offsets[:, start // LIST_ROWS : (start + count) // LIST_ROWS]
+
+        x_bytes = tile([P, TABLE], U8, "x_bytes")
+        nc.vector.memset(x_bytes[:].bitcast(I32)[:, :XS_SPLIT], 0)
+        nc.gpsimd.memset(x_bytes[:].bitcast(I32)[:, XS_SPLIT:], 0)
+        w1_bytes = zeroed_bytes(S, "w1_bytes")
+        d_bytes = zeroed_bytes(TABLE, "d_bytes")
+        w2_bytes = zeroed_bytes(S, "w2_bytes")
+        dk_bytes_placed = zeroed_bytes(S, "dk_bytes_placed")
+        offs_sb = load_list(offs, "offs_sb")
+        k1_sb = load_list(k1, "k1_sb")
+        w1_codes = load_weight_words(w1_words, "w1_codes")
+        load_scale_rows((nc.sync, nc.scalar), x_bytes, x_scales)
+        x_codes = load_table_words(x_words, "x_codes")
+        load_scale_rows((nc.sync,), w1_bytes, w1_scales)
+        row_step = P // (PACK * PACK)
+        nc.sync.dma_start(d_bytes[:].bitcast(I32)[0:P:row_step, :], d_scales[0].bitcast(I32))
+        two_sb = load_list(two, "two_sb")
+        n1_sb = load_list(n1, "n1_sb")
+        d_codes = load_table_words(d_words, "d_codes")
+        n2_sb = load_list(n2, "n2_sb")
+        n3_sb = load_list(n3, "n3_sb")
+        n4_sb = load_list(n4, "n4_sb")
         gain = tile([P, PACK], F32, "gain")
         nc.sync.dma_start(gain[:], gn.rearrange("(p t) o -> p (t o)", t=PACK))
-        w2w = load_fp4(w2_words, "w2w")
-        n5_t = load_list(n5, "n5_t")
-        load_scale_rows((nc.sync,), w2s, w2_scales)
+        w2_codes = load_weight_words(w2_words, "w2_codes")
+        n5_sb = load_list(n5, "n5_sb")
+        load_scale_rows((nc.sync,), w2_bytes, w2_scales)
 
-        h = [tile([P, S], F32, "h%d" % t) for t in range(PACK)]
+        half_h = [tile([P, S], F32, "half_h%d" % t) for t in range(PACK)]
 
-        w1w_d = deal(w1w, U16, "w1w_d")
-        x1s = gather(xs, offs_t, U8, "x1s")
-        x1w = gather(xw, offs_t, U32, "x1w")
-        w1s_d = deal(w1s, U8, "w1s_d")
+        w1_codes_dealt = deal(w1_codes, U16, "w1_codes_dealt")
+        x1_bytes = gather_packed(x_bytes, offs_sb, U8, "x1_bytes")
+        x1_codes = gather_packed(x_codes, offs_sb, U32, "x1_codes")
+        w1_bytes_dealt = deal(w1_bytes, U8, "w1_bytes_dealt")
         y = []
         for t in range(PACK):
             bank = psum.tile([P, S], F32, name="bank_a%d" % t)
-            nc.tensor.matmul_mx(
-                out=bank[:], lhsT=w1w_d[:, P * t : P * (t + 1)].bitcast(FP4X4), lhsT_scale=w1s_d[:, P * t : P * (t + 1)],
-                rhs=x1w[:].bitcast(FP8X4), rhs_scale=x1s[:], start=True, stop=True,
-            )
+            product(bank[:], w1_codes_dealt, FP4X4, w1_bytes_dealt, t, x1_codes, x1_bytes)
             y_t = tile([P, S], F32, "y%d" % t)
             nc.scalar.activation(y_t[:], bank[:], ACT.Copy)
             y.append(y_t)
 
-        dks = gather(ds, k1_t, U8, "dks")
-        dks_d = deal(dks, U8, "dks_d")
+        dk_bytes = gather_packed(d_bytes, k1_sb, U8, "dk_bytes")
+        dk_bytes_dealt = deal(dk_bytes, U8, "dk_bytes_dealt")
         for a in range(PACK):
-            nc.sync.dma_start(dks_p[:].bitcast(I32)[a:P:32, :], dks_d[:].bitcast(I32)[8 * a : P : 32, :])
-        x2s = gather(xs, two_t, U8, "x2s")
-        x2w = gather(xw, two_t, U32, "x2w")
-        dkw = gather(dw, k1_t, U32, "dkw")
-        dkw_d = deal(dkw, U32, "dkw_d")
-        w2w_d = deal(w2w, U16, "w2w_d", "dkw")
-        w2s_d = deal(w2s, U8, "w2s_d", "dw")
+            nc.sync.dma_start(
+                dk_bytes_placed[:].bitcast(I32)[a:P:QUADRANT, :],
+                dk_bytes_dealt[:].bitcast(I32)[row_step * a : P : QUADRANT, :],
+            )
+        x2_bytes = gather_packed(x_bytes, two_sb, U8, "x2_bytes")
+        x2_codes = gather_packed(x_codes, two_sb, U32, "x2_codes")
+        dk_codes = gather_packed(d_codes, k1_sb, U32, "dk_codes")
+        dk_codes_dealt = deal(dk_codes, U32, "dk_codes_dealt")
+        w2_codes_dealt = deal(w2_codes, U16, "w2_codes_dealt", "dk_codes")
+        w2_bytes_dealt = deal(w2_bytes, U8, "w2_bytes_dealt", "d_codes")
         d = []
         for t in range(PACK):
             bank = psum.tile([P, S], F32, name="bank_b%d" % t)
-            nc.tensor.matmul_mx(
-                out=bank[:], lhsT=dkw_d[:, P * t : P * (t + 1)].bitcast(FP8X4), lhsT_scale=dks_p[:, P * t : P * (t + 1)],
-                rhs=x2w[:].bitcast(FP8X4), rhs_scale=x2s[:], start=True, stop=True,
-            )
+            product(bank[:], dk_codes_dealt, FP8X4, dk_bytes_placed, t, x2_codes, x2_bytes)
             d_t = tile([P, S], F32, "d%d" % t)
             nc.vector.tensor_scalar(d_t[:], bank[:], 0.0625, None, ALU.mult)
             d.append(d_t)
 
-        units = [(c, t) for c in range(len(Z_CHUNKS)) for t in range(PACK)]
-        picked = {}
+        steps = [(c, t) for c in range(len(Z_CHUNKS)) for t in range(PACK)]
+        y_picked, d_picked = {}, {}
         z_rows = [tile([P, PACK, width], BF16, "z_rows%d" % c) for c, (start, width) in enumerate(Z_CHUNKS)]
 
-        def columns(offsets, start, count):
-            return offsets[:, start // 16 : (start + count) // 16]
+        def scalar_gathers(table, lists, start, width, name):
+            dst = tile([P, 2, width], F32, name)
+            for e, offsets in enumerate(lists):
+                nc.scalar.activation(dst[:, e, :], table[:].indirect(entries(offsets, start, width)), ACT.Copy)
+            return dst
 
-        def pick_y(c, t):
+        def pick_for_z(step):
+            c, t = steps[step]
             start, width = Z_CHUNKS[c]
-            g = tile([P, 2, width], F32, "ypick%d_%d" % (c, t))
-            for e, offsets in enumerate((n1_t, n2_t)):
-                nc.scalar.activation(g[:, e, :], y[t][:].indirect(columns(offsets, start, width)), ACT.Copy)
-            picked[c, t] = g
-            if PACK * c + t >= FUSED_UNITS:
-                g = tile([P, 2, width], F32, "dpick%d_%d" % (c, t))
-                for e, offsets in enumerate((n3_t, n4_t)):
-                    nc.scalar.activation(g[:, e, :], d[t][:].indirect(columns(offsets, start, width)), ACT.Copy)
-                picked[c, t, "d"] = g
+            y_picked[step] = scalar_gathers(y[t], (n1_sb, n2_sb), start, width, "y_picked%d" % step)
+            if step >= FUSED_STEPS:
+                d_picked[step] = scalar_gathers(d[t], (n3_sb, n4_sb), start, width, "d_picked%d" % step)
 
-        def make_z(c, t):
+        def make_z(step):
+            c, t = steps[step]
             start, width = Z_CHUNKS[c]
-            sums = tile([P, 2, width], F32, "sums%d_%d" % (c, t))
-            if (c, t, "d") in picked:
-                nc.vector.tensor_tensor(sums[:], picked[c, t, "d"][:], picked[c, t][:], ALU.add)
+            sums = tile([P, 2, width], F32, "sums%d" % step)
+            if step >= FUSED_STEPS:
+                nc.vector.tensor_tensor(sums[:], d_picked[step][:], y_picked[step][:], ALU.add)
             else:
-                for e, offsets in enumerate((n3_t, n4_t)):
-                    nc.vector.tensor_tensor(sums[:, e, :], d[t][:].indirect(columns(offsets, start, width)), picked[c, t][:, e, :], ALU.add)
-            top = tile([P, width], F32, "top%d_%d" % (c, t))
-            nc.vector.tensor_tensor(top[:], sums[:, 0, :], sums[:, 1, :], ALU.max)
-            nc.scalar.activation(z_rows[c][:, t, :], top[:], ACT.Copy, scale=gain[:, t : t + 1])
+                for e, offsets in enumerate((n3_sb, n4_sb)):
+                    looked_up = d[t][:].indirect(entries(offsets, start, width))
+                    nc.vector.tensor_tensor(sums[:, e, :], looked_up, y_picked[step][:, e, :], ALU.add)
+            larger = tile([P, width], F32, "larger%d" % step)
+            nc.vector.tensor_tensor(larger[:], sums[:, 0, :], sums[:, 1, :], ALU.max)
+            nc.scalar.activation(z_rows[c][:, t, :], larger[:], ACT.Copy, scale=gain[:, t : t + 1])
 
         def make_h(c):
             start, width = Z_CHUNKS[c]
             z_in = tile([P, width, PACK], BF16, "z_in%d" % c)
             interleave(z_in, z_rows[c])
-            zw = tile([P, width], U32, "zw%d" % c)
-            zs = tile([P, width], U8, "zs%d" % c)
-            nc.vector.quantize_mx(out=zw[:].bitcast(FP8X4), scales=zs[:], in_=z_in[:].rearrange("p j t -> p (j t)"))
+            z_codes = tile([P, width], U32, "z_codes%d" % c)
+            z_bytes = tile([P, width], U8, "z_bytes%d" % c)
+            nc.vector.quantize_mx(
+                out=z_codes[:].bitcast(FP8X4), scales=z_bytes[:], in_=z_in[:].rearrange("p j t -> p (j t)")
+            )
             for t in range(PACK):
-                bank = psum.tile([P, S], F32, name="bank_%s%d" % ("ab"[c % 2], t))
-                nc.tensor.matmul_mx(
-                    out=bank[:, :width], lhsT=w2w_d[:, P * t : P * (t + 1)].bitcast(FP4X4), lhsT_scale=w2s_d[:, P * t : P * (t + 1)],
-                    rhs=zw[:].bitcast(FP8X4), rhs_scale=zs[:], start=True, stop=True,
-                )
+                bank = psum.tile([P, S], F32, name="bank_%s%d" % ("ab"[c], t))
+                product(bank[:, :width], w2_codes_dealt, FP4X4, w2_bytes_dealt, t, z_codes, z_bytes)
                 if c == len(Z_CHUNKS) - 1 and t < VECTOR_BANKS:
-                    nc.vector.tensor_scalar(h[t][:, start : start + width], bank[:, :width], 0.5, None, ALU.mult)
+                    nc.vector.tensor_scalar(half_h[t][:, start : start + width], bank[:, :width], 0.5, None, ALU.mult)
                 else:
-                    nc.scalar.activation(h[t][:, start : start + width], bank[:, :width], ACT.Copy, scale=0.5)
+                    nc.scalar.activation(half_h[t][:, start : start + width], bank[:, :width], ACT.Copy, scale=0.5)
 
-        ahead = 2
-        for u in range(ahead):
-            pick_y(*units[u])
-        for u, (c, t) in enumerate(units):
-            if u + ahead < len(units):
-                pick_y(*units[u + ahead])
-            make_z(c, t)
+        for step in range(PICK_AHEAD):
+            pick_for_z(step)
+        for step in range(len(steps)):
+            if step + PICK_AHEAD < len(steps):
+                pick_for_z(step + PICK_AHEAD)
+            make_z(step)
         for c in range(len(Z_CHUNKS)):
             make_h(c)
 
         out_rows = out_0.rearrange("(p t) j -> p t j", t=PACK)
         out_words = out_1[0].rearrange("p c r -> p (c r)").bitcast(I32)
-        ow = tile([P, S], U32, "ow")
-        osc = tile([P, S], U8, "osc")
-        last = len(OUT_CHUNKS) - 1
-        units = [(c, 0, PACK) for c in range(last + 1)]
+        out_codes = tile([P, S], U32, "out_codes")
+        out_bytes = tile([P, S], U8, "out_bytes")
         result = [tile([P, PACK, width], F32, "result%d" % c) for c, (start, width) in enumerate(OUT_CHUNKS)]
         members = {}
 
-        def pick_h(u):
-            c, first, count = units[u]
+        def pick_members(c):
             start, width = OUT_CHUNKS[c]
-            mb = ring.tile([P, count, 2 * width], F32, name="mb", align_bytes=64, bufs=2)
-            for i in range(count):
-                window = h[first + i][:].indirect(columns(n5_t, 2 * start, 2 * width))
-                if u == 0 and i < VECTOR_PICKS:
-                    nc.vector.tensor_copy(mb[:, i, :], window)
+            picked = ring.tile([P, PACK, 2 * width], F32, name="picked", align_bytes=64, bufs=2)
+            for t in range(PACK):
+                looked_up = half_h[t][:].indirect(entries(n5_sb, 2 * start, 2 * width))
+                if c == 0 and t < VECTOR_PICKS:
+                    nc.vector.tensor_copy(picked[:, t, :], looked_up)
                 else:
-                    nc.scalar.activation(mb[:, i, :], window, ACT.Copy)
-            members[u] = mb
+                    nc.scalar.activation(picked[:, t, :], looked_up, ACT.Copy)
+            members[c] = picked
 
-        def gate(u):
-            c, first, count = units[u]
+        def factors(c):
             start, width = OUT_CHUNKS[c]
-            pairs = members[u][:].rearrange("p t (j e) -> p e t j", e=2)
-            high = ring.tile([P, count, width], F32, name="high", align_bytes=64)
-            low = ring.tile([P, count, width], F32, name="low", align_bytes=64)
+            pairs = members[c][:].rearrange("p t (j e) -> p e t j", e=2)
+            high = ring.tile([P, PACK, width], F32, name="high", align_bytes=64)
+            low = ring.tile([P, PACK, width], F32, name="low", align_bytes=64)
             nc.vector.tensor_tensor(low[:], pairs[:, 0], pairs[:, 1], ALU.min)
             nc.vector.tensor_tensor(high[:], pairs[:, 0], pairs[:, 1], ALU.max)
-            sig = ring.tile([P, count, width], F32, name="sig", align_bytes=64)
-            nc.scalar.activation(sig[:], high[:], ACT.Tanh)
-            rest = ring.tile([P, count, width], F32, name="rest", align_bytes=64)
-            for i in range(count):
-                nc.vector.tensor_tensor(rest[:, i, :], h[first + i][:, start : start + width], low[:, i, :], ALU.subtract)
-            return rest, sig
-
-        def finish(u, rest, sig):
-            c, first, count = units[u]
-            nc.vector.scalar_tensor_tensor(result[c][:, first : first + count, :], sig[:], 1.0, rest[:], ALU.add, ALU.mult)
+            tanh_high = ring.tile([P, PACK, width], F32, name="tanh_high", align_bytes=64)
+            nc.scalar.activation(tanh_high[:], high[:], ACT.Tanh)
+            rest = ring.tile([P, PACK, width], F32, name="rest", align_bytes=64)
+            for t in range(PACK):
+                nc.vector.tensor_tensor(rest[:, t, :], half_h[t][:, start : start + width], low[:, t, :], ALU.subtract)
+            return tanh_high, rest
 
         def hand_out(c):
             start, width = OUT_CHUNKS[c]
             cols = slice(start, start + width)
             nc.sync.dma_start(out_rows[:, :, cols], result[c][:])
-            o_in = tile([P, width, PACK], BF16, "o_in%d" % c)
-            interleave(o_in, result[c])
-            nc.vector.quantize_mx(out=ow[:, cols].bitcast(FP8X4), scales=osc[:, cols], in_=o_in[:].rearrange("p j t -> p (j t)"))
-            nc.sync.dma_start(out_words[:, cols], ow[:, cols].bitcast(I32))
+            out_in = tile([P, width, PACK], BF16, "out_in%d" % c)
+            interleave(out_in, result[c])
+            nc.vector.quantize_mx(
+                out=out_codes[:, cols].bitcast(FP8X4), scales=out_bytes[:, cols], in_=out_in[:].rearrange("p j t -> p (j t)")
+            )
+            nc.sync.dma_start(out_words[:, cols], out_codes[:, cols].bitcast(I32))
 
-        pick_h(0)
-        for u, (c, first, count) in enumerate(units):
-            if u + 1 < len(units):
-                pick_h(u + 1)
-            made = gate(u)
-            if first == 0 and c > 0:
+        pick_members(0)
+        for c in range(len(OUT_CHUNKS)):
+            if c + 1 < len(OUT_CHUNKS):
+                pick_members(c + 1)
+            tanh_high, rest = factors(c)
+            if c > 0:
                 hand_out(c - 1)
-            finish(u, *made)
-        hand_out(last)
+            nc.vector.scalar_tensor_tensor(result[c][:], tanh_high[:], 1.0, rest[:], ALU.add, ALU.mult)
+        hand_out(len(OUT_CHUNKS) - 1)
         for q in range(PACK):
             queue = nc.sync if q % 2 else nc.scalar
-            queue.dma_start(out_2[0].bitcast(I32)[PACK * q : PACK * (q + 1), :], osc[:].bitcast(I32)[32 * q : 32 * q + PACK, :])
+            queue.dma_start(
+                out_2[0].bitcast(I32)[PACK * q : PACK * (q + 1), :],
+                out_bytes[:].bitcast(I32)[QUADRANT * q : QUADRANT * q + PACK, :],
+            )

from contextlib import ExitStack

import concourse.mybir as mybir

F32 = mybir.dt.float32
BF16 = mybir.dt.bfloat16
I32 = mybir.dt.int32
U32 = mybir.dt.uint32
U16 = mybir.dt.uint16
U8 = mybir.dt.uint8
FP8X4 = mybir.dt.float8_e4m3fn_x4
FP4X4 = mybir.dt.float4_e2m1fn_x4
ALU = mybir.AluOpType
ACT = mybir.ActivationFunctionType

P = 128
PACK = 4
QUADRANT = 32
LIST_ROWS = 16
TABLE = 2048
S = 512

Z_CHUNKS = ((0, 256), (256, 256))
OUT_CHUNKS = ((0, 128), (128, 128), (256, 128), (384, 64), (448, 64))

XS_SPLIT = 320
FUSED_STEPS = 5
VECTOR_BANKS = 2
VECTOR_PICKS = 2
PICK_AHEAD = 2

FLOPS = 3 * 2 * 512 * 512 * 512


def tile_picked_twkeypathbghard_none_po_kernel(
    tc, x_words, x_scales, w1_words, w1_scales, d_words, d_scales, gn, w2_words, w2_scales,
    offs, k1, two, n1, n2, n3, n4, n5, out_0, out_1, out_2,
):
    nc = tc.nc
    with ExitStack() as ctx:
        held = ctx.enter_context(tc.tile_pool(name="held", bufs=1))
        ring = ctx.enter_context(tc.tile_pool(name="ring", bufs=3))
        psum = ctx.enter_context(tc.psum_pool(name="psum", bufs=1))

        def tile(shape, dtype, name, tag=None):
            return held.tile(shape, dtype, name=name, tag=tag or name, align_bytes=64)

        def load_list(src, name):
            dst = tile([P, src.shape[1]], U16, name)
            nc.sync.dma_start(dst[:], src)
            return dst

        def zeroed_bytes(width, name):
            dst = tile([P, width], U8, name)
            nc.vector.memset(dst[:].bitcast(I32), 0)
            return dst

        def load_scale_rows(queues, dst, src):
            for a in range(PACK):
                queues[a % len(queues)].dma_start(
                    dst[:].bitcast(I32)[a:P:QUADRANT, :], src[0].bitcast(I32)[a : PACK * PACK : PACK, :]
                )

        def load_table_words(src, name):
            dst = tile([P, TABLE], U32, name)
            nc.sync.dma_start(dst[:].bitcast(I32), src[0].rearrange("p c r -> p (c r)").bitcast(I32))
            return dst

        def load_weight_words(src, name):
            dst = tile([P, S], U16, name)
            nc.sync.dma_start(dst[:].bitcast(I32), src[0].bitcast(I32))
            return dst

        def gather_packed(table, offsets, dtype, name):
            dst = tile([P, S], dtype, name)
            nc.vector.tensor_copy(dst[:], table[:].indirect(offsets[:]))
            return dst

        def deal(src, dtype, name, tag=None):
            dst = tile([P, S], dtype, name, tag)
            nc.vector.tensor_copy(
                dst[:].rearrange("p (t m) -> p t m", t=PACK),
                src[:].rearrange("p (m t) -> p t m", t=PACK),
            )
            return dst

        def interleave(dst, src):
            nc.vector.tensor_copy(
                dst[:].rearrange("p (c i) t -> p c t i", i=PACK), src[:].rearrange("p t (c i) -> p c t i", i=PACK)
            )

        def product(out, words, dtype, scales, t, rhs_words, rhs_scales):
            nc.tensor.matmul_mx(
                out=out, lhsT=words[:, P * t : P * (t + 1)].bitcast(dtype), lhsT_scale=scales[:, P * t : P * (t + 1)],
                rhs=rhs_words[:].bitcast(FP8X4), rhs_scale=rhs_scales[:], start=True, stop=True,
            )

        def entries(offsets, start, count):
            return offsets[:, start // LIST_ROWS : (start + count) // LIST_ROWS]

        x_bytes = tile([P, TABLE], U8, "x_bytes")
        nc.vector.memset(x_bytes[:].bitcast(I32)[:, :XS_SPLIT], 0)
        nc.gpsimd.memset(x_bytes[:].bitcast(I32)[:, XS_SPLIT:], 0)
        w1_bytes = zeroed_bytes(S, "w1_bytes")
        d_bytes = zeroed_bytes(TABLE, "d_bytes")
        w2_bytes = zeroed_bytes(S, "w2_bytes")
        dk_bytes_placed = zeroed_bytes(S, "dk_bytes_placed")
        offs_sb = load_list(offs, "offs_sb")
        k1_sb = load_list(k1, "k1_sb")
        w1_codes = load_weight_words(w1_words, "w1_codes")
        load_scale_rows((nc.sync, nc.scalar), x_bytes, x_scales)
        x_codes = load_table_words(x_words, "x_codes")
        load_scale_rows((nc.sync,), w1_bytes, w1_scales)
        row_step = P // (PACK * PACK)
        nc.sync.dma_start(d_bytes[:].bitcast(I32)[0:P:row_step, :], d_scales[0].bitcast(I32))
        two_sb = load_list(two, "two_sb")
        n1_sb = load_list(n1, "n1_sb")
        d_codes = load_table_words(d_words, "d_codes")
        n2_sb = load_list(n2, "n2_sb")
        n3_sb = load_list(n3, "n3_sb")
        n4_sb = load_list(n4, "n4_sb")
        gain = tile([P, PACK], F32, "gain")
        nc.sync.dma_start(gain[:], gn.rearrange("(p t) o -> p (t o)", t=PACK))
        w2_codes = load_weight_words(w2_words, "w2_codes")
        n5_sb = load_list(n5, "n5_sb")
        load_scale_rows((nc.sync,), w2_bytes, w2_scales)

        half_h = [tile([P, S], F32, "half_h%d" % t) for t in range(PACK)]

        w1_codes_dealt = deal(w1_codes, U16, "w1_codes_dealt")
        x1_bytes = gather_packed(x_bytes, offs_sb, U8, "x1_bytes")
        x1_codes = gather_packed(x_codes, offs_sb, U32, "x1_codes")
        w1_bytes_dealt = deal(w1_bytes, U8, "w1_bytes_dealt")
        y = []
        for t in range(PACK):
            bank = psum.tile([P, S], F32, name="bank_a%d" % t)
            product(bank[:], w1_codes_dealt, FP4X4, w1_bytes_dealt, t, x1_codes, x1_bytes)
            y_t = tile([P, S], F32, "y%d" % t)
            nc.scalar.activation(y_t[:], bank[:], ACT.Copy)
            y.append(y_t)

        dk_bytes = gather_packed(d_bytes, k1_sb, U8, "dk_bytes")
        dk_bytes_dealt = deal(dk_bytes, U8, "dk_bytes_dealt")
        for a in range(PACK):
            nc.sync.dma_start(
                dk_bytes_placed[:].bitcast(I32)[a:P:QUADRANT, :],
                dk_bytes_dealt[:].bitcast(I32)[row_step * a : P : QUADRANT, :],
            )
        x2_bytes = gather_packed(x_bytes, two_sb, U8, "x2_bytes")
        x2_codes = gather_packed(x_codes, two_sb, U32, "x2_codes")
        dk_codes = gather_packed(d_codes, k1_sb, U32, "dk_codes")
        dk_codes_dealt = deal(dk_codes, U32, "dk_codes_dealt")
        w2_codes_dealt = deal(w2_codes, U16, "w2_codes_dealt", "dk_codes")
        w2_bytes_dealt = deal(w2_bytes, U8, "w2_bytes_dealt", "d_codes")
        d = []
        for t in range(PACK):
            bank = psum.tile([P, S], F32, name="bank_b%d" % t)
            product(bank[:], dk_codes_dealt, FP8X4, dk_bytes_placed, t, x2_codes, x2_bytes)
            d_t = tile([P, S], F32, "d%d" % t)
            nc.vector.tensor_scalar(d_t[:], bank[:], 0.0625, None, ALU.mult)
            d.append(d_t)

        steps = [(c, t) for c in range(len(Z_CHUNKS)) for t in range(PACK)]
        y_picked, d_picked = {}, {}
        z_rows = [tile([P, PACK, width], BF16, "z_rows%d" % c) for c, (start, width) in enumerate(Z_CHUNKS)]

        def scalar_gathers(table, lists, start, width, name):
            dst = tile([P, 2, width], F32, name)
            for e, offsets in enumerate(lists):
                nc.scalar.activation(dst[:, e, :], table[:].indirect(entries(offsets, start, width)), ACT.Copy)
            return dst

        def pick_for_z(step):
            c, t = steps[step]
            start, width = Z_CHUNKS[c]
            y_picked[step] = scalar_gathers(y[t], (n1_sb, n2_sb), start, width, "y_picked%d" % step)
            if step >= FUSED_STEPS:
                d_picked[step] = scalar_gathers(d[t], (n3_sb, n4_sb), start, width, "d_picked%d" % step)

        def make_z(step):
            c, t = steps[step]
            start, width = Z_CHUNKS[c]
            sums = tile([P, 2, width], F32, "sums%d" % step)
            if step >= FUSED_STEPS:
                nc.vector.tensor_tensor(sums[:], d_picked[step][:], y_picked[step][:], ALU.add)
            else:
                for e, offsets in enumerate((n3_sb, n4_sb)):
                    looked_up = d[t][:].indirect(entries(offsets, start, width))
                    nc.vector.tensor_tensor(sums[:, e, :], looked_up, y_picked[step][:, e, :], ALU.add)
            larger = tile([P, width], F32, "larger%d" % step)
            nc.vector.tensor_tensor(larger[:], sums[:, 0, :], sums[:, 1, :], ALU.max)
            nc.scalar.activation(z_rows[c][:, t, :], larger[:], ACT.Copy, scale=gain[:, t : t + 1])

        def make_h(c):
            start, width = Z_CHUNKS[c]
            z_in = tile([P, width, PACK], BF16, "z_in%d" % c)
            interleave(z_in, z_rows[c])
            z_codes = tile([P, width], U32, "z_codes%d" % c)
            z_bytes = tile([P, width], U8, "z_bytes%d" % c)
            nc.vector.quantize_mx(
                out=z_codes[:].bitcast(FP8X4), scales=z_bytes[:], in_=z_in[:].rearrange("p j t -> p (j t)")
            )
            for t in range(PACK):
                bank = psum.tile([P, S], F32, name="bank_%s%d" % ("ab"[c], t))
                product(bank[:, :width], w2_codes_dealt, FP4X4, w2_bytes_dealt, t, z_codes, z_bytes)
                if c == len(Z_CHUNKS) - 1 and t < VECTOR_BANKS:
                    nc.vector.tensor_scalar(half_h[t][:, start : start + width], bank[:, :width], 0.5, None, ALU.mult)
                else:
                    nc.scalar.activation(half_h[t][:, start : start + width], bank[:, :width], ACT.Copy, scale=0.5)

        for step in range(PICK_AHEAD):
            pick_for_z(step)
        for step in range(len(steps)):
            if step + PICK_AHEAD < len(steps):
                pick_for_z(step + PICK_AHEAD)
            make_z(step)
        for c in range(len(Z_CHUNKS)):
            make_h(c)

        out_rows = out_0.rearrange("(p t) j -> p t j", t=PACK)
        out_words = out_1[0].rearrange("p c r -> p (c r)").bitcast(I32)
        out_codes = tile([P, S], U32, "out_codes")
        out_bytes = tile([P, S], U8, "out_bytes")
        result = [tile([P, PACK, width], F32, "result%d" % c) for c, (start, width) in enumerate(OUT_CHUNKS)]
        members = {}

        def pick_members(c):
            start, width = OUT_CHUNKS[c]
            picked = ring.tile([P, PACK, 2 * width], F32, name="picked", align_bytes=64, bufs=2)
            for t in range(PACK):
                looked_up = half_h[t][:].indirect(entries(n5_sb, 2 * start, 2 * width))
                if c == 0 and t < VECTOR_PICKS:
                    nc.vector.tensor_copy(picked[:, t, :], looked_up)
                else:
                    nc.scalar.activation(picked[:, t, :], looked_up, ACT.Copy)
            members[c] = picked

        def factors(c):
            start, width = OUT_CHUNKS[c]
            pairs = members[c][:].rearrange("p t (j e) -> p e t j", e=2)
            high = ring.tile([P, PACK, width], F32, name="high", align_bytes=64)
            low = ring.tile([P, PACK, width], F32, name="low", align_bytes=64)
            nc.vector.tensor_tensor(low[:], pairs[:, 0], pairs[:, 1], ALU.min)
            nc.vector.tensor_tensor(high[:], pairs[:, 0], pairs[:, 1], ALU.max)
            tanh_high = ring.tile([P, PACK, width], F32, name="tanh_high", align_bytes=64)
            nc.scalar.activation(tanh_high[:], high[:], ACT.Tanh)
            rest = ring.tile([P, PACK, width], F32, name="rest", align_bytes=64)
            for t in range(PACK):
                nc.vector.tensor_tensor(rest[:, t, :], half_h[t][:, start : start + width], low[:, t, :], ALU.subtract)
            return tanh_high, rest

        def hand_out(c):
            start, width = OUT_CHUNKS[c]
            cols = slice(start, start + width)
            nc.sync.dma_start(out_rows[:, :, cols], result[c][:])
            out_in = tile([P, width, PACK], BF16, "out_in%d" % c)
            interleave(out_in, result[c])
            nc.vector.quantize_mx(
                out=out_codes[:, cols].bitcast(FP8X4), scales=out_bytes[:, cols], in_=out_in[:].rearrange("p j t -> p (j t)")
            )
            nc.sync.dma_start(out_words[:, cols], out_codes[:, cols].bitcast(I32))

        pick_members(0)
        for c in range(len(OUT_CHUNKS)):
            if c + 1 < len(OUT_CHUNKS):
                pick_members(c + 1)
            tanh_high, rest = factors(c)
            if c > 0:
                hand_out(c - 1)
            nc.vector.scalar_tensor_tensor(result[c][:], tanh_high[:], 1.0, rest[:], ALU.add, ALU.mult)
        hand_out(len(OUT_CHUNKS) - 1)
        for q in range(PACK):
            queue = nc.sync if q % 2 else nc.scalar
            queue.dma_start(
                out_2[0].bitcast(I32)[PACK * q : PACK * (q + 1), :],
                out_bytes[:].bitcast(I32)[QUADRANT * q : QUADRANT * q + PACK, :],
            )
